import numpy as np
import ml_dtypes


def mxq(x, axis, fmt="e4m3"):
    dtype, down = {"e4m3": (ml_dtypes.float8_e4m3fn, 7), "e5m2": (ml_dtypes.float8_e5m2, 14)}[fmt]
    v = np.moveaxis(np.asarray(x, np.float32).astype(ml_dtypes.bfloat16).astype(np.float64), axis, -1)
    blocks = v.reshape(v.shape[:-1] + (-1, 32))
    amax = np.abs(blocks).max(-1, keepdims=True)
    byte = np.maximum(np.where(amax > 0, np.frexp(amax)[1] - 1 + 127, 0) - down, 1)
    scale = np.exp2(byte - 127.0)
    codes = (blocks / scale).astype(np.float32).astype(dtype).astype(np.float64)
    return np.moveaxis((codes * scale).reshape(v.shape), -1, axis)


WIDE = False


def mx_kscale(k):
    if not WIDE:
        return np.ones(k)
    levels = np.array([10, -10, 5, -5, 0])
    if k % 512:
        return np.exp2(np.random.permutation(np.resize(levels, k // 32))).repeat(32)
    a = np.empty((k // 512, 16))
    for p in range(k // 512):
        a[p, :8] = np.random.permutation(np.resize(levels, 8))
        for g in range(8):
            far = levels[np.abs(levels - a[p, g]) >= 10]
            a[p, g + 8] = far[np.random.randint(len(far))]
    return np.exp2(a.ravel()).repeat(32)


BF16 = ml_dtypes.bfloat16


def bf(x):
    return np.asarray(x, np.float32).astype(BF16)


def f64(x):
    return np.asarray(x).astype(np.float64)

def planes(Y):
    n, m = Y.shape
    b = f64(bf(Y)).reshape(n // 32, 32, m)
    amax = np.abs(b).max(1)
    byte = np.clip(np.where(amax > 0, np.frexp(amax)[1] - 1 + 127 - 7, 1), 1, 254)
    codes = (b * np.exp2(127.0 - byte)[:, None, :]).reshape(n, m).astype(np.float32).astype(ml_dtypes.float8_e4m3fn).view(np.uint8)
    words = codes.reshape(n // 512, 128, 4, m).transpose(0, 1, 3, 2)
    return np.ascontiguousarray(words), np.ascontiguousarray(byte.astype(np.uint8).reshape(n // 512, 16, m))


T, D, I, J, O = 1024, 512, 4, 4, 128
M = I * J + I * J + I


def logsumexp(c, axis):
    m = c.max(axis=axis, keepdims=True)
    return m + np.log(np.sum(np.exp(c - m), axis=axis, keepdims=True))


def softmax(c, axis):
    e = np.exp(c - c.max(axis=axis, keepdims=True))
    return e / np.sum(e, axis=axis, keepdims=True)


def project(x, g, w):
    d, m, o = w.shape
    p = mxq(x * g[None, :], 1, "e4m3") @ mxq(w.reshape(d, m * o), 0, "e4m3")
    return p.reshape(x.shape[0], m, o)


def setup_inputs():
    kd = mx_kscale(D)
    kt = mx_kscale(T)
    return {
        "x": bf(np.random.standard_normal((T, D))),
        "g": bf((1.0 + 0.1 * np.random.standard_normal(D)) * kd),
        "w": bf(np.random.standard_normal((D, M, O)) / np.sqrt(D) / kd[:, None, None]),
        "y": bf(np.random.standard_normal((T, O)) * 1.2),
        "s": bf(np.random.standard_normal((I, J, O)) * 0.4),
        "u": bf((1.0 + 0.1 * np.random.standard_normal(T)) / kt),
        "q": bf((1.0 + 0.1 * np.random.standard_normal(T)) * kt),
    }


def core(x, g, w, y, s, u, q):
    x, g, w, y, s, u, q = f64(x), f64(g), f64(w), f64(y), f64(s), f64(u), f64(q)
    t, d = x.shape
    ni, nj, o = s.shape
    n = ni * nj

    p = project(x, g, w)

    mu = p[:, :n].reshape(t, ni, nj, o)
    c = p[:, n:n + n].reshape(t, ni, nj, o)
    a = p[:, n + n:]

    lg2 = c - logsumexp(c, 2)

    r = y[:, None, None, :] - mu
    v = np.exp(-s)[None]
    joint = a[:, :, None, :] + lg2 - 0.5 * (s[None] + r ** 2 * v)

    h = softmax(joint, (1, 2))
    gm = h * r * v * q[:, None, None, None]

    xu = x * u[:, None]
    dw = (mxq(np.transpose(xu), 1, "e4m3") @ mxq(gm.reshape(t, n * o), 0, "e4m3")) / 8.0
    return dw.reshape(d, ni, nj, o)


def reference(x, g, w, y, s, u, q):
    R_out = core(x, g, w, y, s, u, q)
    words, scales = planes(np.moveaxis(R_out, 0, 0).reshape(512, -1))
    return R_out, words, scales

import math
from contextlib import ExitStack

import concourse.mybir as mybir
from concourse.masks import make_identity

T, D, NI, NJ, O = 1024, 512, 4, 4, 128
FLOPS = 2 * T * D * 36 * O + 2 * D * T * NI * NJ * O

F32 = mybir.dt.float32
BF16 = mybir.dt.bfloat16
U32 = mybir.dt.uint32
I32 = mybir.dt.int32
U8 = mybir.dt.uint8
FP8X4 = mybir.dt.float8_e4m3fn_x4
ALU = mybir.AluOpType
ACT = mybir.ActivationFunctionType

P = 128
BLOCK = 256
N_BLOCKS = T // BLOCK
R_SLOTS = 14
SCORE_SLOTS = 6
E_SLOTS = 5
FLIP_BANKS = 4
TOP_GATE_CHUNK = 8
POOL_Y = False
POOL_SHIFT = False
ONE_PORT = False
POOL_XU = False
W_ENG = "vvsssvsss"


ORDER = """
turn_x:0 gain_x:0 turn_y interleave_w:0:0 copy_y interleave_w:4:0 turn_x:1 quantize_w:0 quantize_w:4
quantize_x:0 turn_s interleave_w:8:1 halve_s project_means:0:0 gain_x:1 quantize_x:1 exp_s quantize_w:8
interleave_w:2:0 project_gates:0:0 negate_gates:0:0 scale_s gate_max_a:0:0 gate_max_b:0:0 interleave_w:5:1
turn_x:2 interleave_w:1:0 turn_x:3 residual:0:0 quantize_w:5 square:0:0 gate_flips:0:0:0 gate_offset:0:0
quantize_w:2 gain_x:2 quantize_w:1 project_gates:0:1 scores:0:0 quantize_x:2 negate_gates:0:1 gate_max_a:0:1
project_means:0:1 gain_x:3 residual:0:1 project_means:0:2 score_min_a:0:0 gate_max_b:0:1 quantize_x:3
interleave_w:6:1 score_min_b:0:0 square:0:1 scores:0:1 gate_flips:0:0:1 quantize_w:6 gate_offset:0:1
project_gates:0:2 score_min_a:0:1 gate_flips:0:1:0 gate_flips:0:1:1 interleave_w:7:1 residual:0:2
gate_exp:0:0:0 negate_gates:0:2 quantize_w:7 interleave_w:3:0 gate_max_a:0:2 score_min_b:0:1 gate_exp:0:0:1
gate_max_b:0:2 gate_offset:0:2 project_gates:0:3 gate_flips:0:2:1 gate_flips:0:2:0 quantize_w:3 square:0:2
project_means:0:3 gate_exp:0:1:0 gate_exp:0:1:1 scores:0:2 residual:0:3 negate_gates:0:3 score_min_a:0:2
gate_max_a:0:3 score_min_b:0:2 project_means:1:0 gate_exp:0:2:0 gate_max_b:0:3 residual:1:0 gate_flips:0:3:1
square:0:3 gate_offset:0:3 project_means:1:1 gate_exp:0:2:1 square:1:0 project_gates:1:0 negate_gates:1:0
scores:0:3 score_min_a:0:3 gate_flips:0:3:0 gate_exp:0:3:0 residual:1:1 sum_gates:0:0 gate_exp:0:3:1
gate_max_a:1:0 score_min_b:0:3 log_gates:0:0 gate_max_b:1:0 scores:1:0 project_means:1:2 sum_gates:0:1
log_gates:0:1 gate_offset:1:0 project_gates:1:1 score_min_a:1:0 residual:1:2 project_means:1:3
negate_gates:1:1 gate_flips:1:0:0 shift:0:0 gate_max_a:1:1 shift:0:1 square:1:1 gate_max_b:1:1 shift:0:2
gate_offset:1:1 gate_flips:1:1:0 gate_exp:1:0:0 gate_flips:1:0:1 shift:0:3 scores:1:1 shift:0:4
project_gates:1:2 gate_exp:1:1:0 gate_flips:1:1:1 gate_exp:1:0:1 negate_gates:1:2 score_min_b:1:0
gate_exp:1:1:1 gate_max_a:1:2 gate_max_b:1:2 score_min_a:1:1 joint_flips:0:0:0 joint_flips:0:0:1
gate_offset:1:2 joint_flips:0:1:0 joint_exp:0:0:0 square:1:2 joint_exp:0:0:1 score_min_b:1:1 project_gates:1:3
gate_flips:1:2:0 scores:1:2 joint_flips:0:1:1 residual:1:3 negate_gates:1:3 gate_flips:1:2:1 gate_max_a:1:3
score_min_a:1:2 joint_exp:0:1:0 gate_max_b:1:3 gate_offset:1:3 project_means:2:0 project_gates:2:0
residual:2:0 project_means:2:1 joint_exp:0:1:1 gate_exp:1:2:0 joint_flips:0:2:0 square:1:3 joint_flips:0:2:1
score_min_b:1:2 negate_gates:2:0 gate_max_a:2:0 gate_exp:1:2:1 joint_exp:0:2:0 gate_flips:1:3:0
joint_flips:0:3:0 scores:1:3 gate_flips:1:3:1 gate_max_b:2:0 residual:2:1 square:2:0 scores:2:0
score_min_a:1:3 score_min_b:1:3 gate_exp:1:3:0 joint_exp:0:2:1 joint_exp:0:3:0 project_means:2:2
gate_exp:1:3:1 joint_flips:0:3:1 sum_gates:1:0 square:2:1 gate_offset:2:0 gate_flips:2:0:0 sum_gates:1:1
residual:2:2 project_gates:2:1 joint_exp:0:3:1 log_gates:1:0 log_gates:1:1 gate_flips:2:0:1 score_min_a:2:0
score_min_b:2:0 negate_gates:2:1 gate_exp:2:0:0 project_means:2:3 sum_joint:0 shift:1:0 gate_exp:2:0:1
gate_max_a:2:1 shift:1:1 gate_max_b:2:1 shift:1:2 gate_offset:2:1 project_gates:2:2 shift:1:3 scores:2:1
log_total:0 negate_gates:2:2 gate_flips:2:1:0 shift:1:4 joint_flips:1:0:0 invert_total:0 residual:2:3
score_min_a:2:1 project_means:3:0 gate_max_a:2:2 joint_flips:1:0:1 joint_exp:1:0:0 gate_flips:2:1:1
gate_max_b:2:2 joint_exp:1:0:1 residual:3:0 project_means:3:1 gate_exp:2:1:0 gate_offset:2:2 weigh_total:0
project_gates:2:3 residual:3:1 joint_flips:1:1:0 square:2:2 weigh_residual:0:1:3 negate_gates:2:3
weigh_residual:0:1:2 gate_exp:2:1:1 joint_flips:1:1:1 scores:2:2 gate_max_a:2:3 weigh_residual:0:2:3
joint_exp:1:1:1 joint_exp:1:1:0 weigh_residual:0:3:1 score_min_b:2:1 weigh_residual:0:2:0 gate_flips:2:2:0
project_means:3:2 gate_exp:2:2:0 square:2:3 joint_flips:1:2:0 gate_max_b:2:3 gate_flips:2:2:1
weigh_residual:0:2:2 joint_flips:1:2:1 scores:2:3 score_min_a:2:2 gate_offset:2:3 gate_flips:2:3:0
weigh_residual:0:0:0 gate_exp:2:2:1 project_gates:3:0 joint_exp:1:2:0 joint_flips:1:3:0 weigh_residual:0:1:1
gate_flips:2:3:1 joint_exp:1:2:1 negate_gates:3:0 weigh_residual:0:0:2 gate_exp:2:3:0 square:3:0
joint_flips:1:3:1 weigh_residual:0:1:0 gate_max_a:3:0 weigh_residual:0:0:1 gate_exp:2:3:1 sum_gates:2:0
gate_max_b:3:0 joint_exp:1:3:0 joint_exp:1:3:1 log_gates:2:0 score_min_b:2:2 score_min_a:2:3 scores:3:0
sum_gates:2:1 score_min_b:2:3 score_min_a:3:0 gate_offset:3:0 sum_joint:1 weigh_residual:0:3:2 log_gates:2:1
project_gates:3:1 weigh_residual:0:3:3 log_total:1 invert_total:1 score_min_b:3:0 gate_flips:3:0:0
weigh_residual:0:0:3 negate_gates:3:1 weigh_residual:0:2:1 weigh_residual:0:3:0 shift:2:0 shift:2:1
gate_flips:3:0:1 shift:2:2 shift:2:3 weigh_total:1 shift:2:4 weigh_residual:1:1:2 gate_exp:3:0:0
weigh_residual:1:0:0 joint_flips:2:0:0 gate_max_a:3:1 square:3:1 gate_exp:3:0:1 joint_exp:2:0:0
weigh_residual:1:0:3 scores:3:1 gate_max_b:3:1 joint_flips:2:0:1 weigh_residual:1:0:1 joint_exp:2:0:1
gate_offset:3:1 project_gates:3:2 weigh_residual:1:1:1 negate_gates:3:2 gate_flips:3:1:0 score_min_a:3:1
gate_max_a:3:2 turn_residual:0:0:0 gate_flips:3:1:1 gate_exp:3:1:0 weigh_residual:1:0:2 turn_residual:0:0:1
gate_max_b:3:2 score_min_b:3:1 gate_offset:3:2 turn_residual:0:0:2 gradient:0:0:0 gradient:0:0:1
turn_residual:0:0:3 residual:3:2 gate_exp:3:1:1 project_gates:3:3 joint_flips:2:1:0 gradient:0:0:2
gradient:0:0:3 gate_flips:3:2:0 joint_flips:2:1:1 square:3:2 scores:3:2 negate_gates:3:3 joint_exp:2:1:0
project_means:3:3 quantize_gradient:0:0:0:4 weigh_residual:1:1:0 gate_flips:3:2:1 gate_exp:3:2:0
joint_exp:2:1:1 gate_max_a:3:3 turn_residual:0:1:0 weigh_residual:1:3:0 score_min_a:3:2 gate_max_b:3:3
gate_exp:3:2:1 weigh_residual:1:2:0 gradient:0:1:0 turn_residual:0:1:1 weigh_residual:1:1:3 gradient:0:1:1
gate_flips:3:3:0 turn_residual:0:1:2 turn_residual:0:1:3 joint_flips:2:2:0 residual:3:3 gradient:0:1:3
gate_exp:3:3:0 gradient:0:1:2 square:3:3 gate_flips:3:3:1 joint_exp:2:2:0 turn_residual:0:2:0
weigh_residual:1:3:1 weigh_residual:1:2:1 score_min_b:3:2 gate_offset:3:3 joint_flips:2:2:1 gate_exp:3:3:1
joint_exp:2:2:1 sum_gates:3:0 weigh_residual:1:2:3 scores:3:3 turn_residual:0:2:1 gradient:0:2:0 sum_gates:3:1
log_gates:3:0 reload_x:1 score_min_a:3:3 weigh_residual:1:2:2 quantize_gradient:0:1:0:4 score_min_b:3:3
log_gates:3:1 gradient:0:2:1 turn_residual:0:2:2 turn_residual:0:2:3 gradient:0:2:2 gradient:0:2:3
joint_flips:2:3:1 joint_flips:2:3:0 reload_x:0 shift:3:0 joint_exp:2:3:0 quantize_gradient:0:2:0:4
joint_exp:2:3:1 turn_residual:0:3:0 shift:3:1 weigh_residual:1:3:2 shift:3:2 weigh_residual:1:3:3 sum_joint:2
shift:3:3 gradient:0:3:0 shift:3:4 weigh_x:0 turn_residual:0:3:1 joint_flips:3:0:0 turn_residual:0:3:3
log_total:2 gradient:0:3:1 turn_residual:0:3:2 gradient:0:3:3 joint_flips:3:0:1 joint_exp:3:0:0 gradient:0:3:2
joint_flips:3:1:1 invert_total:2 joint_flips:3:2:0 weigh_total:2 quantize_gradient:0:3:0:4
weigh_residual:2:0:1 joint_exp:3:0:1 joint_flips:3:1:0 joint_exp:3:2:0 joint_exp:3:1:1 joint_flips:3:3:0
joint_exp:3:1:0 weigh_residual:2:2:3 weigh_residual:2:0:2 joint_flips:3:2:1 weigh_x:1 weigh_residual:2:3:0
joint_flips:3:3:1 joint_exp:3:3:0 joint_exp:3:2:1 weigh_residual:2:0:3 joint_exp:3:3:1 weigh_residual:2:2:0
weigh_residual:2:1:0 quantize_xu:0 sum_joint:3 weigh_residual:2:0:0 reciprocal_total:3 weigh_residual:2:2:1
weigh_total:3 weigh_residual:2:1:1 weigh_residual:3:0:0 turn_residual:1:0:0 quantize_xu:1 weigh_residual:3:0:3
turn_residual:1:0:3 weigh_residual:3:0:1 turn_residual:1:0:1 weigh_residual:2:1:3 weigh_residual:3:1:0
gradient:1:0:0 weigh_residual:3:0:2 quantize_gradient:1:0:0:1 contract:0:0 turn_residual:1:1:0
turn_residual:1:0:2 weigh_residual:2:2:2 gradient:1:0:1 round_result:0:0 weigh_residual:3:1:2
quantize_gradient:1:0:1:2 copy_result:0:0 weigh_residual:2:3:1 weigh_residual:2:1:2 weigh_residual:2:3:3
gradient:1:0:2 contract:0:1 gradient:1:0:3 quantize_gradient:1:0:2:3 contract:0:2 weigh_residual:3:1:1
copy_result:0:1 weigh_residual:3:1:3 turn_residual:1:1:1 gradient:1:1:0 quantize_gradient:1:0:3:4 contract:0:3
round_result:0:2 weigh_residual:3:2:2 round_result:0:1 turn_residual:1:1:2 gradient:1:1:1 copy_result:0:2
quantize_gradient:1:1:0:1 weigh_residual:2:3:2 contract:1:0 copy_result:0:3 weigh_residual:3:2:0
gradient:1:1:2 copy_result:1:0 turn_residual:1:1:3 round_result:0:3 quantize_gradient:1:1:1:2
turn_residual:1:2:0 weigh_residual:3:2:1 weigh_residual:3:2:3 store_result:0 quantize_gradient:1:1:2:3
turn_residual:1:2:1 contract:1:1 gradient:1:1:3 round_result:1:0 copy_result:1:1 turn_residual:1:2:2
quantize_result:0 contract:1:2 round_result:1:1 quantize_gradient:1:1:3:4 contract:1:3 gradient:1:2:0
copy_result:1:2 round_result:1:3 round_result:1:2 copy_result:1:3 gradient:1:2:1 quantize_gradient:1:2:0:1
contract:2:0 gradient:1:2:2 quantize_gradient:1:2:1:2 turn_residual:1:2:3 weigh_residual:3:3:0 contract:2:1
quantize_gradient:1:2:2:3 turn_residual:1:3:0 copy_result:2:0 contract:2:2 weigh_residual:3:3:1
round_result:2:0 round_result:2:1 store_result:1 copy_result:2:1 quantize_result:1 gradient:1:2:3
gradient:1:3:0 quantize_gradient:1:2:3:4 weigh_residual:3:3:2 round_result:2:2 weigh_residual:3:3:3
turn_residual:1:3:1 contract:2:3 gradient:1:3:1 copy_result:2:2 copy_result:2:3 quantize_gradient:1:3:0:1
turn_residual:1:3:2 round_result:2:3 store_codes:0 turn_residual:1:3:3 quantize_gradient:1:3:1:2
gradient:1:3:2 contract:3:0 copy_result:3:0 quantize_result:2 round_result:3:0 store_codes:1
quantize_gradient:1:3:2:3 store_codes:2 contract:3:1 gradient:1:3:3 copy_result:3:1 contract:3:2
round_result:3:1 quantize_gradient:1:3:3:4 store_result:2 contract:3:3 copy_result:3:2 round_result:3:3
copy_result:3:3 round_result:3:2 quantize_result:3 store_result:3 store_scales:2 store_scales:3 store_codes:3
store_scales:1 store_scales:0
"""


def program():
    return [[w.split(":")[0]] + [int(a) for a in w.split(":")[1:]] for w in ORDER.split()]


def tile_hierarchicalmixtureeffectiveweightgradie_kernel(tc, x, g, w, y, s, u, q, out_0, out_1, out_2):
    nc = tc.nc
    with ExitStack() as ctx:
        sb = ctx.enter_context(tc.tile_pool(name="sb", bufs=1))
        ps = ctx.enter_context(tc.psum_pool(name="ps", bufs=1))
        ctx.enter_context(tc.manual_schedule())

        def sbuf(shape, dtype, tag):
            return sb.tile(shape, dtype, name=tag, tag=tag, align_bytes=64)

        def bank(shape, tag, dtype=F32):
            return ps.tile(shape, dtype, name=tag, tag=tag)

        flips_taken = []

        def flip_bank(shape, dtype=F32):
            flips_taken.append(1)
            return bank(shape, "flip%d" % (len(flips_taken) % FLIP_BANKS), dtype)

        def stage_tile(shape, n):
            return sbuf(shape, BF16, "stage%d" % (n % 2))

        def flip_sum(out, parts):
            for n, part in enumerate(parts):
                nc.tensor.matmul(out, part, ident[:], start=(n == 0), stop=(n == len(parts) - 1), is_transpose=True)

        def mx(out, lhs, lhs_cols, rhs, rhs_cols, start, stop):
            nc.tensor.matmul_mx(out=out, lhsT=lhs[0][:, lhs_cols].bitcast(FP8X4), lhsT_scale=lhs[1][:, lhs_cols],
                                rhs=rhs[0][:, rhs_cols].bitcast(FP8X4), rhs_scale=rhs[1][:, rhs_cols],
                                start=start, stop=stop)

        def quantize(dst, cols, src):
            nc.vector.quantize_mx(out=dst[0][:, cols].bitcast(FP8X4), scales=dst[1][:, cols], in_=src)

        def cols(n, width=P):
            return slice(n * width, (n + 1) * width)

        ident = sbuf([P, P], F32, "ident")
        ident_bf = sbuf([P, P], BF16, "ident_bf")
        s_rows = sbuf([P, P], BF16, "s_rows")
        nc.gpsimd.memset(s_rows[:], 0.0)
        make_identity(nc, ident[:])
        make_identity(nc, ident_bf[:])

        x_view = x.rearrange("(g p t) d -> g p t d", g=2, t=4)
        w_view = w.rearrange("(p j) m o -> p j (m o)", j=4)
        x_sb = [sbuf([P, 4, D], BF16, tag) for tag in ("score5", "r13")]
        g_sb = sbuf([P, 4], BF16, "g")
        u_sb = sbuf([P, 2, 4], BF16, "u")
        y_sb = sbuf([P, 2, 4, O], BF16, "e4")
        q_sb = sbuf([P, T], BF16, "q")
        chunk_order = [0, 4, TOP_GATE_CHUNK, 1, 5, 2, 6, 3, 7]
        w_raw = {}

        def load_w(chunk):
            w_raw[chunk] = sbuf([P, 4, 512], BF16, "r%d" % (4 + chunk_order.index(chunk)))
            nc.sync.dma_start(out=w_raw[chunk][:], in_=w_view[:, :, cols(chunk, 512)])

        nc.sync.dma_start(out=x_sb[0][:], in_=x_view[0])
        nc.scalar.dma_start(out=g_sb[:], in_=g.rearrange("(p j) -> p j", j=4))
        nc.scalar.dma_start(out=s_rows[0:16, :], in_=s.rearrange("i j o -> (i j) o"))
        load_w(0)
        nc.sync.dma_start(out=y_sb[:], in_=y.rearrange("(g p t) o -> p g t o", g=2, t=4))
        for chunk in chunk_order[1:]:
            load_w(chunk)
        nc.sync.dma_start(out=x_sb[1][:], in_=x_view[1])
        nc.sync.dma_start(out=u_sb[:], in_=u.rearrange("(g p t) -> p g t", g=2, t=4))
        nc.sync.dma_start(out=q_sb[:], in_=q.partition_broadcast(P))

        w_mx = (sbuf([P, 36 * O], U32, "w_codes"), sbuf([P, 36 * O], U8, "w_scales"))
        xg_mx = (sbuf([P, T], U32, "xg_codes"), sbuf([P, T], U8, "xg_scales"))
        xu_mx = (sbuf([P, 2 * D], U32, "xu_codes"), sbuf([P, 2 * D], U8, "xu_scales"))
        w_il = {}

        def interleave_w(chunk, unused):
            on_scalar = W_ENG[chunk_order.index(chunk)] == "s"
            il = sbuf([P, 512, 4], BF16, "e%d" % (chunk_order.index(chunk) % 4))
            w_il[chunk] = il
            src = w_raw[chunk][:].rearrange("p j (c e) -> p c j e", e=4)
            dst = il[:].rearrange("p (c e) j -> p c j e", e=4)
            first = 32 if 4 <= chunk < TOP_GATE_CHUNK else 0
            if on_scalar:
                if first:
                    nc.scalar.activation(out=dst[:, :first], in_=src[:, :first], func=ACT.Copy, scale=-1.0)
                nc.scalar.copy(out=dst[:, first:], in_=src[:, first:])
            else:
                if first:
                    nc.vector.tensor_scalar(out=dst[:, :first], in0=src[:, :first], scalar1=-1.0, scalar2=None, op0=ALU.mult)
                nc.vector.tensor_copy(out=dst[:, first:], in_=src[:, first:])

        def quantize_w(chunk):
            quantize(w_mx, cols(chunk, 512), w_il[chunk][:].rearrange("p c j -> p (c j)"))

        xg_il, x_turned, small = {}, {}, {}

        def turn_x(b):
            words = x_sb[b // 2][:].bitcast(F32)
            x_turned[b] = flip_bank([P, 2, 2, P])
            for h in range(2):
                for t in range(2):
                    nc.tensor.transpose(x_turned[b][:, h, t, :], words[:, 2 * (b % 2) + t, h::2], ident[:])

        def gain_x(b):
            xg_il[b] = stage_tile([P, BLOCK, 2, 2], b)
            pairs = x_turned[b][:].rearrange("p h t n -> p (h t n)").bitcast(BF16).rearrange("p (h n e) -> p n h e", h=2, e=2)
            gains = g_sb[:].rearrange("p (h e) -> p h e", h=2).unsqueeze(1).broadcast_to([P, BLOCK, 2, 2])
            nc.vector.tensor_tensor(out=xg_il[b][:], in0=pairs, in1=gains, op=ALU.mult)

        def quantize_x(b):
            quantize(xg_mx, cols(b, BLOCK), xg_il[b][:].rearrange("p n h e -> p (n h e)"))

        xu_il, x_again = {}, {}

        def reload_x(grp):
            x_again[grp] = sbuf([P, 4, D], BF16, "gexp%d" % grp)
            nc.sync.dma_start(out=x_again[grp][:], in_=x_view[grp])

        def weigh_x(grp):
            xu_il[grp] = stage_tile([P, 4, P, 4], grp)
            src = x_again[grp][:].rearrange("p t (m r) -> p r m t", r=4)
            weights = u_sb[:, grp, :].unsqueeze(1).unsqueeze(1).broadcast_to([P, 4, P, 4])
            (nc.gpsimd if POOL_XU else nc.vector).tensor_tensor(out=xu_il[grp][:], in0=src, in1=weights, op=ALU.mult)

        def quantize_xu(grp):
            quantize(xu_mx, cols(grp, D), xu_il[grp][:].rearrange("p r m t -> p (r m t)"))

        y_t = sbuf([P, T], BF16, "y_t")
        half_s = sbuf([P, NI, NJ], F32, "half_s")
        rel_s = sbuf([P, NI, NJ], F32, "rel_s")
        v = sbuf([P, NI, NJ], F32, "v")
        root_v = sbuf([P, NI, NJ], F32, "root_v")
        kappa = sbuf([P, NI, NJ], F32, "kappa")

        def turn_s():
            small["s"] = flip_bank([P, P], BF16)
            nc.tensor.transpose(small["s"][:], s_rows[:], ident_bf[:])

        def halve_s():
            s_cols = small["s"][:, 0:16].rearrange("p (i j) -> p i j", j=NJ)
            nc.vector.tensor_scalar(out=half_s[:], in0=s_cols, scalar1=0.5, scalar2=None, op0=ALU.mult)

        def exp_s():
            nc.scalar.activation(out=root_v[:], in_=half_s[:], func=ACT.Exp, scale=-1.0)
            nc.scalar.activation(out=v[:], in_=half_s[:], func=ACT.Exp, scale=-2.0)

        def scale_s():
            nc.vector.tensor_tensor(out=rel_s[:], in0=half_s[:], in1=half_s[:, :, 0:1].broadcast_to([P, NI, NJ]), op=ALU.subtract)
            nc.vector.tensor_scalar(out=kappa[:], in0=root_v[:], scalar1=math.sqrt(0.5), scalar2=None, op0=ALU.mult)

        def turn_y():
            small["y"] = flip_bank([P, 8, P], BF16)
            for n in range(8):
                nc.tensor.transpose(small["y"][:, n, :], y_sb[:, n // 4, n % 4, :], ident_bf[:])

        def copy_y():
            nc.scalar.copy(out=y_t[:], in_=small["y"][:].rearrange("p n t -> p (n t)"))

        means, gates, resid, score, negdiff, gmax, gexp, joint = {}, {}, {}, {}, {}, {}, {}, {}
        offs, lows, factor = {}, {}, {}

        def project_means(b, i):
            means[b, i] = [bank([P, 2, BLOCK], "mean%d" % n) for n in range(2)]
            for j in range(NJ):
                mx(means[b, i][j // 2][:, j % 2, :], w_mx, cols(NJ * i + j), xg_mx, cols(b, BLOCK), True, True)

        def project_gates(b, i):
            gates[b, i] = [bank([P, 2, BLOCK], "gate%d" % n) for n in range(2)]
            for j in range(1, NJ):
                dst = gates[b, i][(j - 1) // 2][:, (j - 1) % 2, :]
                mx(dst, w_mx, cols(16 + NJ * i + j), xg_mx, cols(b, BLOCK), True, False)
                mx(dst, w_mx, cols(16 + NJ * i), xg_mx, cols(b, BLOCK), False, True)
            mx(gates[b, i][1][:, 1, :], w_mx, cols(32 + i), xg_mx, cols(b, BLOCK), True, True)

        def residual(b, i):
            resid[b, i] = sbuf([P, NJ, BLOCK], F32, "r%d" % ((NI * b + i) % R_SLOTS))
            target = y_t[:, cols(b, BLOCK)].unsqueeze(1).broadcast_to([P, 2, BLOCK])
            for n in range(2):
                nc.vector.tensor_tensor(out=resid[b, i][:, cols(n, 2), :], in0=target, in1=means[b, i][n][:], op=ALU.subtract)

        def square(b, i):
            score[b, i] = sbuf([P, NJ, BLOCK], F32, "score%d" % ((NI * b + i) % SCORE_SLOTS))
            for j in (1, 2, 3, 0):
                nc.scalar.activation(out=score[b, i][:, j, :], in_=resid[b, i][:, j, :], func=ACT.Square, scale=kappa[:, i, j:j + 1])

        def negate_gates(b, i):
            negdiff[b, i] = sbuf([P, 3, BLOCK], F32, "negdiff%d" % (i % 2))
            nc.scalar.activation(out=negdiff[b, i][:, 0:2, :], in_=gates[b, i][0][:], func=ACT.Copy, scale=-1.0)
            nc.scalar.activation(out=negdiff[b, i][:, 2, :], in_=gates[b, i][1][:, 0, :], func=ACT.Copy, scale=-1.0)

        def gate_max_a(b, i):
            gmax[b, i] = sbuf([P, 2, BLOCK], F32, "gmax%d" % (i % 2))
            nc.vector.scalar_tensor_tensor(out=gmax[b, i][:, 0, :], in0=negdiff[b, i][:, 0, :], scalar=-1.0, in1=gates[b, i][0][:, 1, :],
                                           op0=ALU.mult, op1=ALU.max)

        def gate_max_b(b, i):
            nc.vector.scalar_tensor_tensor(out=gmax[b, i][:, 1, :], in0=gmax[b, i][:, 0, :], scalar=0.0, in1=gates[b, i][1][:, 0, :],
                                           op0=ALU.max, op1=ALU.max)

        def gate_offset(b, i):
            if i == 0:
                offs[b] = sbuf([P, NI, BLOCK], F32, "offs%d" % (b % 2))
            nc.vector.scalar_tensor_tensor(out=offs[b][:, i, :], in0=gmax[b, i][:, 1, :], scalar=half_s[:, i, 0:1], in1=gates[b, i][1][:, 1, :],
                                           op0=ALU.add, op1=ALU.subtract)

        def scores(b, i):
            for j in range(1, NJ):
                if ONE_PORT:
                    nc.vector.scalar_tensor_tensor(out=score[b, i][:, j, :], in0=score[b, i][:, j, :], scalar=rel_s[:, i, j:j + 1],
                                                   in1=gates[b, i][(j - 1) // 2][:, (j - 1) % 2, :], op0=ALU.add, op1=ALU.subtract)
                else:
                    nc.vector.scalar_tensor_tensor(out=score[b, i][:, j, :], in0=score[b, i][:, j, :], scalar=rel_s[:, i, j:j + 1],
                                                   in1=negdiff[b, i][:, j - 1, :], op0=ALU.add, op1=ALU.add)

        pair = {}

        def score_min(b, i):
            if i == 0:
                lows[b] = sbuf([P, NI, BLOCK], F32, "lows%d" % (b % 2))
            nc.vector.tensor_reduce(out=lows[b][:, i, :], in_=score[b, i][:].rearrange("p j n -> p n j"), axis=mybir.AxisListType.X, op=ALU.min)

        def score_min_a(b, i):
            pair[b, i] = sbuf([P, 2, BLOCK], F32, "pair")
            nc.vector.tensor_tensor(out=pair[b, i][:], in0=score[b, i][:, 0:2, :], in1=score[b, i][:, 2:4, :], op=ALU.min)

        def score_min_b(b, i):
            if i == 0:
                lows[b] = sbuf([P, NI, BLOCK], F32, "lows%d" % (b % 2))
            nc.vector.tensor_tensor(out=lows[b][:, i, :], in0=pair[b, i][:, 0, :], in1=pair[b, i][:, 1, :], op=ALU.min)

        gate_arg, joint_arg = {}, {}

        def gate_flips(b, i, t):
            gate_arg[b, i, t] = flip_bank([P, NJ, O])
            top = gmax[b, i][:, 1, cols(t)]
            flip_sum(gate_arg[b, i, t][:, 0, :], [top])
            for j in range(1, NJ):
                flip_sum(gate_arg[b, i, t][:, j, :], [negdiff[b, i][:, j - 1, cols(t)], top])

        def gate_exp(b, i, t):
            if t == 0:
                gexp[b, i] = sbuf([P, 2, NJ, O], F32, "gexp%d" % i)
            nc.scalar.activation(out=gexp[b, i][:, t], in_=gate_arg[b, i, t][:], func=ACT.Exp, scale=-1.0)

        def joint_flips(b, i, t):
            joint_arg[b, i, t] = flip_bank([P, NJ, O])
            for j in range(NJ):
                flip_sum(joint_arg[b, i, t][:, j, :], [score[b, i][:, j, cols(t)], offs[b][:, i, cols(t)]])

        def joint_exp(b, i, t):
            if b % 2 == 0 and t == 0:
                joint[b // 2, i] = sbuf([P, 4, NJ, O], F32, "e%d" % ((NI * (b // 2) + i) % E_SLOTS))
            nc.scalar.activation(out=joint[b // 2, i][:, 2 * (b % 2) + t], in_=joint_arg[b, i, t][:], func=ACT.Exp, scale=-1.0)

        totals, gate_sums, log_sums = {}, {}, {}

        def sum_joint(b):
            totals[b] = flip_bank([P, BLOCK])
            for t in range(2):
                flip_sum(totals[b][:, cols(t)], [joint[b // 2, i][:, 2 * (b % 2) + t, j, :] for i in range(NI) for j in range(NJ)])

        def sum_gates(b, half):
            gate_sums[b, half] = flip_bank([P, 2, BLOCK])
            for n in range(2):
                for t in range(2):
                    flip_sum(gate_sums[b, half][:, n, cols(t)], [gexp[b, 2 * half + n][:, t, j, :] for j in range(NJ)])

        def log_gates(b, half):
            if half == 0:
                log_sums[b] = sbuf([P, NI, BLOCK], F32, "log_sums")
            nc.scalar.activation(out=log_sums[b][:, cols(half, 2), :], in_=gate_sums[b, half][:], func=ACT.Ln)

        def log_total(b):
            factor[b] = sbuf([P, 2, P], F32, "factor%d" % (b % 2))
            nc.scalar.activation(out=factor[b][:].rearrange("p t n -> p (t n)"), in_=totals[b][:], func=ACT.Ln)

        def invert_total(b):
            nc.scalar.activation(out=factor[b][:], in_=factor[b][:], func=ACT.Exp, scale=-1.0)

        def reciprocal_total(b):
            factor[b] = sbuf([P, 2, P], F32, "factor%d" % (b % 2))
            nc.vector.reciprocal(out=factor[b][:].rearrange("p t n -> p (t n)"), in_=totals[b][:])

        def weigh_total(b):
            weights = q_sb[:, cols(b // 2, 512)].rearrange("p (n t) -> p t n", t=4)[:, cols(b % 2, 2), :]
            nc.vector.tensor_tensor(out=factor[b][:], in0=factor[b][:], in1=weights, op=ALU.mult)

        least = {}

        def shift(b, part):
            eng = nc.gpsimd if POOL_SHIFT else nc.vector
            if part == 0:
                eng.tensor_tensor(out=offs[b][:], in0=offs[b][:], in1=log_sums[b][:], op=ALU.add)
            if part == 1:
                eng.tensor_tensor(out=lows[b][:], in0=lows[b][:], in1=offs[b][:], op=ALU.add)
            if part == 2:
                least[b] = sbuf([P, 2, BLOCK], F32, "least")
                nc.vector.tensor_tensor(out=least[b][:], in0=lows[b][:, 0:2, :], in1=lows[b][:, 2:4, :], op=ALU.min)
            if part == 3:
                nc.vector.tensor_tensor(out=least[b][:, 0, :], in0=least[b][:, 0, :], in1=least[b][:, 1, :], op=ALU.min)
            if part == 4:
                eng.tensor_tensor(out=offs[b][:], in0=offs[b][:], in1=least[b][:, 0:1, :].broadcast_to([P, NI, BLOCK]), op=ALU.subtract)

        def weigh_residual(b, i, j):
            nc.vector.scalar_tensor_tensor(out=resid[b, i][:, j, :], in0=resid[b, i][:, j, :], scalar=v[:, i, j:j + 1],
                                           in1=factor[b][:].rearrange("p t n -> p (t n)"), op0=ALU.mult, op1=ALU.mult)

        def scale_residual(b, i):
            for j in range(NJ):
                nc.gpsimd.tensor_scalar(out=resid[b, i][:, j, :], in0=resid[b, i][:, j, :], scalar1=v[:, i, j:j + 1], scalar2=0.0,
                                        op0=ALU.mult, op1=ALU.add)

        def norm_residual(b, i, half):
            both = factor[b][:].rearrange("p t n -> p (t n)").unsqueeze(1).broadcast_to([P, 2, BLOCK])
            nc.gpsimd.tensor_tensor(out=resid[b, i][:, cols(half, 2), :], in0=resid[b, i][:, cols(half, 2), :], in1=both, op=ALU.mult)

        gm_mx, gm_il, turned = {}, {}, {}

        def turn_residual(grp, i, j):
            turned[grp, i, j] = flip_bank([P, 4, O])
            for t in range(4):
                nc.tensor.transpose(turned[grp, i, j][:, t, :], resid[2 * grp + t // 2, i][:, j, cols(t % 2)], ident[:])

        def gradient(grp, i, j):
            if j == 0:
                gm_il[grp, i] = stage_tile([P, NJ, O, 4], i)
            nc.vector.tensor_tensor(out=gm_il[grp, i][:, j], in0=turned[grp, i, j][:].rearrange("p t o -> p o t"),
                                    in1=joint[grp, i][:, :, j, :].rearrange("p t o -> p o t"), op=ALU.mult)

        def quantize_gradient(grp, i, j0, j1):
            if i == 0 and j0 == 0:
                tag = "w" if grp == 1 else "gm"
                gm_mx[grp] = (sbuf([P, NI * NJ * O], U32, tag + "_codes"), sbuf([P, NI * NJ * O], U8, tag + "_scales"))
            quantize(gm_mx[grp], slice((NJ * i + j0) * O, (NJ * i + j1) * O), gm_il[grp, i][:, j0:j1].rearrange("p j o t -> p (j o t)"))

        result, result_il = {}, {}
        out_view = out_0.rearrange("(m r) i j o -> m r i (j o)", r=4)
        words_view = out_1[0].rearrange("p n t -> p (n t)").bitcast(I32)
        out_scales = sbuf([P, NI * NJ * O], U8, "out_scales")

        sums, codes = {}, {}

        def contract(i, j):
            sums[i, j] = bank([P, 4, O], ("mean0", "mean1", "gate0", "gate1")[j])
            for r in range(4):
                for grp in range(2):
                    mx(sums[i, j][:, r, :], xu_mx, cols(4 * grp + r), gm_mx[grp], cols(NJ * i + j), grp == 0, grp == 1)

        def copy_result(i, j):
            if j == 0:
                result[i] = sbuf([P, 4, NJ, O], F32, "e%d" % ((3 + i) % E_SLOTS))
            nc.scalar.activation(out=result[i][:, :, j, :], in_=sums[i, j][:], func=ACT.Copy, scale=0.125)

        def round_result(i, j):
            if j == 0:
                result_il[i] = sbuf([P, NJ, O, 4], BF16, "score%d" % i)
            nc.scalar.activation(out=result_il[i][:, j], in_=sums[i, j][:].rearrange("p r o -> p o r"), func=ACT.Copy, scale=0.125)

        def store_result(i):
            nc.sync.dma_start(out=out_view[:, :, i, :], in_=result[i][:].rearrange("p r j o -> p r (j o)"))

        def quantize_result(i):
            codes[i] = sbuf([P, NJ * O], U32, "gexp%d" % i)
            nc.vector.quantize_mx(out=codes[i][:].bitcast(FP8X4), scales=out_scales[:, cols(i, 512)],
                                  in_=result_il[i][:].rearrange("p j o r -> p (j o r)"))

        def store_codes(i):
            nc.sync.dma_start(out=words_view[:, cols(i, 512)], in_=codes[i][:].bitcast(I32))

        def store_scales(quad):
            nc.sync.dma_start(out=out_2[0, 4 * quad:4 * quad + 4, :].bitcast(I32), in_=out_scales[32 * quad:32 * quad + 4, :].bitcast(I32))

        steps = dict(interleave_w=interleave_w, quantize_w=quantize_w, turn_x=turn_x, gain_x=gain_x, quantize_x=quantize_x, reload_x=reload_x, weigh_x=weigh_x, quantize_xu=quantize_xu, turn_s=turn_s, halve_s=halve_s, exp_s=exp_s, scale_s=scale_s, turn_y=turn_y, copy_y=copy_y, project_means=project_means, project_gates=project_gates, residual=residual, square=square, negate_gates=negate_gates, gate_max_a=gate_max_a, gate_max_b=gate_max_b, gate_offset=gate_offset, scores=scores, score_min=score_min, score_min_a=score_min_a, score_min_b=score_min_b, gate_flips=gate_flips, gate_exp=gate_exp, joint_flips=joint_flips, joint_exp=joint_exp, sum_joint=sum_joint, sum_gates=sum_gates, log_gates=log_gates, log_total=log_total, invert_total=invert_total, reciprocal_total=reciprocal_total, weigh_total=weigh_total, shift=shift, weigh_residual=weigh_residual, scale_residual=scale_residual, norm_residual=norm_residual, turn_residual=turn_residual, gradient=gradient, quantize_gradient=quantize_gradient, contract=contract, copy_result=copy_result, round_result=round_result, store_result=store_result, quantize_result=quantize_result, store_codes=store_codes, store_scales=store_scales)
        for name, *args in program():
            steps[name](*args)
